import numpy as np
import ml_dtypes

BF16 = ml_dtypes.bfloat16


def bf(x):
    return np.asarray(x, np.float32).astype(BF16)


def f32(x):
    return np.asarray(x, np.float32)


def f64(x):
    return np.asarray(x).astype(np.float64)


def striped(idx):
    return np.concatenate([l.reshape(-1, 16).T for l in idx])


def rows(idx, k):
    return np.tile(np.repeat(idx, 16, axis=0), (k // (16 * 8), 1))


def look(tab, idx):
    return np.take_along_axis(f64(tab), rows(idx, len(tab)), axis=1)


K, S, V, N = 512, 2048, 1024, 1024


def setup_inputs():
    return {"tab": f32(np.random.standard_normal((2, K, S))), "offs": striped(np.stack([np.random.permutation(S)[:N] for _ in range(8)]))}


def reference(tab, offs):
    idx = np.stack([g.T.reshape(-1) for g in np.split(offs, 8)])
    x = (np.minimum(np.maximum(look(tab[0], idx), -1.25), 1.0)) * (np.tanh(look(tab[1], idx)))
    return x

@@ -1,0 +1,34 @@
+import concourse.mybir as mybir
+
+P = 128
+LOW, HIGH = -1.25, 1.0
+F32, U16 = mybir.dt.float32, mybir.dt.uint16
+ALU = mybir.AluOpType
+TANH = mybir.ActivationFunctionType.Tanh
+
+
+def tile_lookup_vg_cliptanh_out_kernel(tc, tab, offs, out):
+    nc = tc.nc
+    rows, places = tab.shape[1], tab.shape[2]
+    picks = out.shape[1]
+    blocks = rows // P
+    with (
+        tc.tile_pool(name="held", bufs=1) as held,
+        tc.tile_pool(name="work", bufs=blocks) as work,
+    ):
+        offsets = held.tile([P, picks // 16], U16, name="offsets")
+        nc.sync.dma_start(offsets[:], offs)
+        values, gates = [], []
+        for b in range(blocks):
+            values.append(held.tile([P, places], F32, name=f"values{b}"))
+            gates.append(held.tile([P, places], F32, name=f"gates{b}"))
+            nc.sync.dma_start(values[b][:], tab[0, b * P : (b + 1) * P, :])
+            nc.sync.dma_start(gates[b][:], tab[1, b * P : (b + 1) * P, :])
+        for b in range(blocks):
+            clamped = work.tile([P, picks], F32, name="clamped")
+            opened = work.tile([P, picks], F32, name="opened")
+            product = work.tile([P, picks], F32, name="product")
+            nc.vector.tensor_scalar(clamped[:], values[b][:].indirect(offsets[:]), LOW, HIGH, ALU.max, ALU.min)
+            nc.scalar.activation(opened[:], gates[b][:].indirect(offsets[:]), TANH)
+            nc.vector.tensor_tensor(product[:], clamped[:], opened[:], ALU.mult)
+            nc.sync.dma_start(out[b * P : (b + 1) * P, :], product[:])

@@ -24,11 +24,20 @@ def tile_lookup_vg_cliptanh_out_kernel(tc, tab, offs, out):
             gates.append(held.tile([P, places], F32, name=f"gates{b}"))
             nc.sync.dma_start(values[b][:], tab[0, b * P : (b + 1) * P, :])
             nc.sync.dma_start(gates[b][:], tab[1, b * P : (b + 1) * P, :])
+        half = picks // 2
         for b in range(blocks):
             clamped = work.tile([P, picks], F32, name="clamped")
             opened = work.tile([P, picks], F32, name="opened")
             product = work.tile([P, picks], F32, name="product")
-            nc.vector.tensor_scalar(clamped[:], values[b][:].indirect(offsets[:]), LOW, HIGH, ALU.max, ALU.min)
-            nc.scalar.activation(opened[:], gates[b][:].indirect(offsets[:]), TANH)
-            nc.vector.tensor_tensor(product[:], clamped[:], opened[:], ALU.mult)
-            nc.sync.dma_start(out[b * P : (b + 1) * P, :], product[:])
+            block_rows = slice(b * P, (b + 1) * P)
+            last = b == blocks - 1
+            for h in range(2):
+                cols = slice(h * half, (h + 1) * half)
+                piece = offsets[:, h * half // 16 : (h + 1) * half // 16]
+                nc.vector.tensor_scalar(clamped[:, cols], values[b][:].indirect(piece), LOW, HIGH, ALU.max, ALU.min)
+                nc.scalar.activation(opened[:, cols], gates[b][:].indirect(piece), TANH)
+                nc.vector.tensor_tensor(product[:, cols], clamped[:, cols], opened[:, cols], ALU.mult)
+                if last:
+                    nc.sync.dma_start(out[block_rows, cols], product[:, cols])
+            if not last:
+                nc.sync.dma_start(out[block_rows, :], product[:])

@@ -17,14 +17,15 @@ def tile_lookup_vg_cliptanh_out_kernel(tc, tab, offs, out):
         tc.tile_pool(name="work", bufs=blocks) as work,
     ):
         offsets = held.tile([P, picks // 16], U16, name="offsets")
-        nc.sync.dma_start(offsets[:], offs)
         values, gates = [], []
         for b in range(blocks):
             values.append(held.tile([P, places], F32, name=f"values{b}"))
             gates.append(held.tile([P, places], F32, name=f"gates{b}"))
             nc.sync.dma_start(values[b][:], tab[0, b * P : (b + 1) * P, :])
+            if b == 0:
+                nc.sync.dma_start(offsets[:], offs)
             nc.sync.dma_start(gates[b][:], tab[1, b * P : (b + 1) * P, :])
-        half = picks // 2
+        half, quarter = picks // 2, picks // 4
         for b in range(blocks):
             clamped = work.tile([P, picks], F32, name="clamped")
             opened = work.tile([P, picks], F32, name="opened")
@@ -36,8 +37,12 @@ def tile_lookup_vg_cliptanh_out_kernel(tc, tab, offs, out):
                 piece = offsets[:, h * half // 16 : (h + 1) * half // 16]
                 nc.vector.tensor_scalar(clamped[:, cols], values[b][:].indirect(piece), LOW, HIGH, ALU.max, ALU.min)
                 nc.scalar.activation(opened[:, cols], gates[b][:].indirect(piece), TANH)
-                nc.vector.tensor_tensor(product[:, cols], clamped[:, cols], opened[:, cols], ALU.mult)
                 if last:
-                    nc.sync.dma_start(out[block_rows, cols], product[:, cols])
+                    for q in range(2 * h, 2 * h + 2):
+                        part = slice(q * quarter, (q + 1) * quarter)
+                        nc.vector.tensor_tensor(product[:, part], clamped[:, part], opened[:, part], ALU.mult)
+                        nc.sync.dma_start(out[block_rows, part], product[:, part])
+                else:
+                    nc.vector.tensor_tensor(product[:, cols], clamped[:, cols], opened[:, cols], ALU.mult)
             if not last:
                 nc.sync.dma_start(out[block_rows, :], product[:])

@@ -24,7 +24,8 @@ def tile_lookup_vg_cliptanh_out_kernel(tc, tab, offs, out):
             nc.sync.dma_start(values[b][:], tab[0, b * P : (b + 1) * P, :])
             if b == 0:
                 nc.sync.dma_start(offsets[:], offs)
-            nc.sync.dma_start(gates[b][:], tab[1, b * P : (b + 1) * P, :])
+            gate_queue = nc.scalar if b < blocks // 2 else nc.sync
+            gate_queue.dma_start(gates[b][:], tab[1, b * P : (b + 1) * P, :])
         half, quarter = picks // 2, picks // 4
         for b in range(blocks):
             clamped = work.tile([P, picks], F32, name="clamped")

import concourse.mybir as mybir

P = 128
LOW, HIGH = -1.25, 1.0
F32, U16 = mybir.dt.float32, mybir.dt.uint16
ALU = mybir.AluOpType
TANH = mybir.ActivationFunctionType.Tanh


def tile_lookup_vg_cliptanh_out_kernel(tc, tab, offs, out):
    nc = tc.nc
    rows, places = tab.shape[1], tab.shape[2]
    picks = out.shape[1]
    blocks = rows // P
    with (
        tc.tile_pool(name="held", bufs=1) as held,
        tc.tile_pool(name="work", bufs=blocks) as work,
    ):
        offsets = held.tile([P, picks // 16], U16, name="offsets")
        values, gates = [], []
        for b in range(blocks):
            values.append(held.tile([P, places], F32, name=f"values{b}"))
            gates.append(held.tile([P, places], F32, name=f"gates{b}"))
            nc.sync.dma_start(values[b][:], tab[0, b * P : (b + 1) * P, :])
            if b == 0:
                nc.sync.dma_start(offsets[:], offs)
            gate_queue = nc.scalar if b < blocks // 2 else nc.sync
            gate_queue.dma_start(gates[b][:], tab[1, b * P : (b + 1) * P, :])
        half, quarter = picks // 2, picks // 4
        for b in range(blocks):
            clamped = work.tile([P, picks], F32, name="clamped")
            opened = work.tile([P, picks], F32, name="opened")
            product = work.tile([P, picks], F32, name="product")
            block_rows = slice(b * P, (b + 1) * P)
            last = b == blocks - 1
            for h in range(2):
                cols = slice(h * half, (h + 1) * half)
                piece = offsets[:, h * half // 16 : (h + 1) * half // 16]
                nc.vector.tensor_scalar(clamped[:, cols], values[b][:].indirect(piece), LOW, HIGH, ALU.max, ALU.min)
                nc.scalar.activation(opened[:, cols], gates[b][:].indirect(piece), TANH)
                if last:
                    for q in range(2 * h, 2 * h + 2):
                        part = slice(q * quarter, (q + 1) * quarter)
                        nc.vector.tensor_tensor(product[:, part], clamped[:, part], opened[:, part], ALU.mult)
                        nc.sync.dma_start(out[block_rows, part], product[:, part])
                else:
                    nc.vector.tensor_tensor(product[:, cols], clamped[:, cols], opened[:, cols], ALU.mult)
            if not last:
                nc.sync.dma_start(out[block_rows, :], product[:])
